import numpy as np
import ml_dtypes


def mxq(x, axis, fmt="e4m3"):
    dtype, down = {"e4m3": (ml_dtypes.float8_e4m3fn, 7), "e5m2": (ml_dtypes.float8_e5m2, 14)}[fmt]
    v = np.moveaxis(np.asarray(x, np.float32).astype(ml_dtypes.bfloat16).astype(np.float64), axis, -1)
    blocks = v.reshape(v.shape[:-1] + (-1, 32))
    amax = np.abs(blocks).max(-1, keepdims=True)
    byte = np.maximum(np.where(amax > 0, np.frexp(amax)[1] - 1 + 127, 0) - down, 1)
    scale = np.exp2(byte - 127.0)
    codes = (blocks / scale).astype(np.float32).astype(dtype).astype(np.float64)
    return np.moveaxis((codes * scale).reshape(v.shape), -1, axis)


WIDE = False


def mx_kscale(k):
    if not WIDE:
        return np.ones(k)
    levels = np.array([10, -10, 5, -5, 0])
    if k % 512:
        return np.exp2(np.random.permutation(np.resize(levels, k // 32))).repeat(32)
    a = np.empty((k // 512, 16))
    for p in range(k // 512):
        a[p, :8] = np.random.permutation(np.resize(levels, 8))
        for g in range(8):
            far = levels[np.abs(levels - a[p, g]) >= 10]
            a[p, g + 8] = far[np.random.randint(len(far))]
    return np.exp2(a.ravel()).repeat(32)


def f64(x):
    return np.asarray(x).astype(np.float64)


def striped(idx):
    return np.tile(idx.reshape(-1, 16).T, (8, 1)).astype(np.uint16)


def unstriped(offs):
    return offs[:16].T.reshape(-1).astype(np.int64)


def pack_weight(w):
    k, n = w.shape
    w = f64(np.asarray(w, np.float32).astype(ml_dtypes.bfloat16)).reshape(k // 32, 32, n)
    amax = np.abs(w).max(1)
    byte = np.clip(np.where(amax > 0, np.frexp(amax)[1] - 1 + 127 - 7, 1), 1, 254)
    scaled = (w * np.exp2(127.0 - byte)[:, None, :]).reshape(k, n).astype(np.float32)
    words = np.ascontiguousarray(scaled.reshape(k // 512, 128, 4, n).transpose(0, 1, 3, 2)).astype(ml_dtypes.float8_e4m3fn).view(np.uint8)
    return words, np.ascontiguousarray(byte.astype(np.uint8).reshape(k // 512, 16, n))


def unpack_weight(words, scales):
    g, p, n, _ = words.shape
    vals = np.ascontiguousarray(words).view(ml_dtypes.float8_e4m3fn).astype(np.float64) * np.repeat(np.exp2(scales.astype(np.float64) - 127.0), 8, axis=1)[..., None]
    return vals.transpose(0, 1, 3, 2).reshape(g * 512, n)


K, T, S, N, H = 512, 2048, 512, 128, 512


def setup_inputs():
    n = np.random.standard_normal
    s = mx_kscale(K)[:, None]
    u = mx_kscale(H)
    packed_xT = pack_weight(n((K, T)) * s)
    return {
        "x_words": packed_xT[0],
        "x_scales": packed_xT[1],
        "w1": (n((K, H)) / np.sqrt(K) / s).astype(np.float32),
        "w2": (n((K, H)) / np.sqrt(K) / s).astype(np.float32),
        "owat": (np.random.uniform(0.0, 1.0, (H, S))).astype(np.float32),
        "unit": (np.random.uniform(0.6, 1.4, (H, 1)) * u[:, None]).astype(np.float32),
        "w3": (n((H, N)) / np.sqrt(H) / u[:, None]).astype(np.float32),
        "offs": striped(np.random.permutation(T)[:S]),
        "est": striped(np.random.permutation(S)),
        "nor": striped(np.random.permutation(S)),
    }


def reference(x_words, x_scales, w1, w2, owat, unit, w3, offs, est, nor):
    xq = unpack_weight(x_words, x_scales)[:, unstriped(offs)]
    hi = mxq(f64(w1), 0, "e4m3").T @ xq
    thk = np.log(np.exp(hi) + 1.0)
    pres = thk * (np.exp(-1.0 * f64(owat)))
    ui = mxq(f64(w2), 0, "e4m3").T @ xq
    uu = np.tanh(ui)
    ue = uu[:, unstriped(est)]
    epa = ue - uu
    un = uu[:, unstriped(nor)]
    epb = un - uu
    delta = np.sqrt((epa) ** 2 + 0.25 * ((epb) ** 2) + 0.05)
    zeta = pres / delta
    sig1 = zeta * epa - (0.5 * pres)
    sig2 = 0.25 * (zeta * epb)
    hid = f64(unit) * (sig1 + 1.5 * sig2)
    return mxq(f64(w3), 0, "e4m3").T @ mxq(hid, 0, "e4m3")

@@ -1,0 +1,267 @@
+from contextlib import ExitStack
+
+import concourse.mybir as mybir
+from concourse.masks import make_identity
+
+K, T, S, N, H = 512, 2048, 512, 128, 512
+FLOPS = 2 * K * H * S * 2 + 2 * H * N * S
+
+F32 = mybir.dt.float32
+BF16 = mybir.dt.bfloat16
+I32 = mybir.dt.int32
+U32 = mybir.dt.uint32
+U16 = mybir.dt.uint16
+U8 = mybir.dt.uint8
+FP8X4 = mybir.dt.float8_e4m3fn_x4
+ACT = mybir.ActivationFunctionType
+ALU = mybir.AluOpType
+
+P = 128
+PACK = 4
+HALF = S // 2
+SOFTPLUS_LINEAR_FROM = 40.0
+
+
+def tile_picked_yseaic_str_p_kernel(
+    tc, x_words, x_scales, w1, w2, owat, unit, w3, offs, est, nor, out
+):
+    nc = tc.nc
+    with ExitStack() as ctx:
+        sb = ctx.enter_context(tc.tile_pool(name="sb", bufs=1))
+        psum = ctx.enter_context(tc.psum_pool(name="psum", bufs=1))
+
+        def tile(name, shape, dtype):
+            return sb.tile(shape, dtype, name=name, align_bytes=64)
+
+        def bank(number, name):
+            return psum.tile([P, 512], F32, name=name, tag="bank%d" % number)
+
+        def mx(dst, lhs, rhs):
+            nc.tensor.matmul_mx(
+                out=dst,
+                lhsT=lhs[0].bitcast(FP8X4),
+                lhsT_scale=lhs[1],
+                rhs=rhs[0].bitcast(FP8X4),
+                rhs_scale=rhs[1],
+                start=True,
+                stop=True,
+            )
+
+        def quantize(name, grouped, width):
+            codes = tile(name + "_codes", [P, width], U32)
+            scales = tile(name + "_scales", [P, width], U8)
+            nc.vector.quantize_mx(out=codes[:].bitcast(FP8X4), scales=scales[:], in_=grouped)
+            return codes, scales
+
+        offs_sb = tile("offs_sb", [P, S // 16], U16)
+        est_sb = tile("est_sb", [P, S // 16], U16)
+        nor_sb = tile("nor_sb", [P, S // 16], U16)
+        xw = tile("xw", [P, T], U32)
+        xs = tile("xs", [P, T], U8)
+        nc.gpsimd.memset(xs[:].bitcast(I32), 0)
+        nc.sync.dma_start(offs_sb[:], offs)
+        w2_view = w2.rearrange("(p j) c -> p j c", j=PACK)
+        w2_raw = []
+
+        def load_w2(number, c0, c1):
+            raw = tile("w2_raw%d" % number, [P, PACK, c1 - c0], F32)
+            nc.sync.dma_start(raw[:], w2_view[:, :, c0:c1])
+            for c in range(0, c1 - c0, P):
+                w2_raw.append(raw[:, :, c : c + P])
+
+        load_w2(0, 0, P)
+        for q in range(4):
+            nc.sync.dma_start(xs[32 * q : 32 * q + 4, :].bitcast(I32), x_scales[0, 4 * q : 4 * q + 4, :].bitcast(I32))
+        nc.sync.dma_start(xw[:].bitcast(I32), x_words[0].rearrange("p n t -> p (n t)").bitcast(I32))
+        load_w2(1, P, 2 * P)
+        load_w2(2, 2 * P, H)
+        nc.sync.dma_start(est_sb[:], est)
+        nc.sync.dma_start(nor_sb[:], nor)
+        owat_sb = tile("owat_sb", [P, PACK, S], F32)
+        nc.sync.dma_start(owat_sb[:], owat.rearrange("(p t) j -> p t j", t=PACK))
+        w1_view = w1.rearrange("(p j) c -> p j c", j=PACK)
+        w1_raw = []
+        for h in range(2):
+            raw = tile("w1_raw%d" % h, [P, PACK, H // 2], F32)
+            nc.sync.dma_start(raw[:], w1_view[:, :, h * (H // 2) : (h + 1) * (H // 2)])
+            w1_raw.append(raw)
+        w3_raw = tile("w3_raw", [P, PACK, N], F32)
+        nc.sync.dma_start(w3_raw[:], w3.rearrange("(p j) c -> p j c", j=PACK))
+        unit_sb = tile("unit_sb", [P, PACK], F32)
+        nc.sync.dma_start(unit_sb[:], unit.rearrange("(p t) o -> p (t o)", t=PACK))
+
+        ident = tile("ident", [P, P], F32)
+        make_identity(nc, ident[:])
+
+        xg_scales = tile("xg_scales", [P, S], U8)
+        xg_codes = tile("xg_codes", [P, S], U32)
+        nc.vector.tensor_copy(xg_scales[:], xs[:].indirect(offs_sb[:]))
+        nc.vector.tensor_copy(xg_codes[:], xw[:].indirect(offs_sb[:]))
+        xg = (xg_codes[:], xg_scales[:])
+
+        def group_rows(engine_copy, name, raw, width):
+            grouped = tile(name, [P, width * PACK], BF16)
+            engine_copy(
+                grouped[:].rearrange("p (c e j) -> p c j e", e=2, j=PACK),
+                raw.rearrange("p j (c e) -> p c j e", e=2),
+            )
+            return grouped
+
+        uu, uu_copy = [], []
+        for b in range(4):
+            copy = nc.scalar.copy if b == 0 else nc.vector.tensor_copy
+            grouped = group_rows(copy, "w2_grouped%d" % b, w2_raw[b], P)
+            codes, scales = quantize("w2q%d" % b, grouped[:], P)
+            ui = bank(b, "ui%d" % b)
+            mx(ui[:], (codes[:], scales[:]), xg)
+            u = tile("uu%d" % b, [P, S], F32)
+            nc.scalar.activation(u[:], ui[:], ACT.Tanh)
+            u2 = tile("uu_copy%d" % b, [P, S], F32)
+            nc.vector.tensor_copy(u2[:], u[:])
+            uu.append(u)
+            uu_copy.append(u2)
+
+        def entries(h):
+            return slice(h * HALF // 16, (h + 1) * HALF // 16)
+
+        def strains(h, b, on_scalar):
+            cols = slice(h * HALF, (h + 1) * HALF)
+            epa = tile("epa%d_%d" % (h, b), [P, HALF], F32)
+            epb = tile("epb%d_%d" % (h, b), [P, HALF], F32)
+            nc.vector.tensor_tensor(epa[:], uu[b][:].indirect(est_sb[:, entries(h)]), uu_copy[b][:, cols], ALU.subtract)
+            if on_scalar:
+                un = tile("un%d_%d" % (h, b), [P, HALF], F32)
+                nc.scalar.activation(un[:], uu[b][:].indirect(nor_sb[:, entries(h)]), ACT.Copy, scale=0.375)
+                nc.vector.scalar_tensor_tensor(epb[:], uu[b][:, cols], -0.375, un[:], ALU.mult, ALU.add)
+                strain[h, b] = (epa, epb, 0.5 / 0.375, [epa, epb])
+                return
+            nc.vector.tensor_tensor(epb[:], uu[b][:].indirect(nor_sb[:, entries(h)]), uu_copy[b][:, cols], ALU.subtract)
+            num = tile("num%d_%d" % (h, b), [P, HALF], F32)
+            nc.vector.scalar_tensor_tensor(num[:], epb[:], 0.375, epa[:], ALU.mult, ALU.add)
+            strain[h, b] = (epa, epb, 0.5, [num])
+
+        def squares(h, b):
+            epa, epb, scale, terms = strain[h, b]
+            sqa = tile("sqa%d_%d" % (h, b), [P, HALF], F32)
+            sqb = tile("sqb%d_%d" % (h, b), [P, HALF], F32)
+            nc.scalar.activation(sqa[:], epa[:], ACT.Square)
+            nc.scalar.activation(sqb[:], epb[:], ACT.Square, scale=scale)
+            squared[h, b] = (sqa, sqb)
+
+        def turn(dst, src, start, stop):
+            nc.tensor.matmul(dst, src, ident[:], start=start, stop=stop, is_transpose=True)
+
+        def turned_sums(c):
+            h, cols = c // 2, slice((c % 2) * P, (c % 2 + 1) * P)
+            d2 = bank(2 * c, "d2_%d" % c)
+            num_t = bank(2 * c + 1, "num_t%d" % c)
+            for b in range(4):
+                terms = strain[h, b][3]
+                for number, term in enumerate(terms):
+                    turn(num_t[:, b * P : (b + 1) * P], term[:, cols], number == 0, number == len(terms) - 1)
+            for b in range(4):
+                sqa, sqb = squared[h, b]
+                turn(d2[:, b * P : (b + 1) * P], sqa[:, cols], True, False)
+                turn(d2[:, b * P : (b + 1) * P], sqb[:, cols], False, True)
+            sums.append((d2, num_t))
+
+        strain, squared, sums, hi = {}, {}, [], []
+        w1_grouped = tile("w1_grouped", [P, PACK, P, PACK], BF16)
+        exp_hi = tile("exp_hi", [P, PACK, S], F32)
+        open_water = tile("open_water", [P, PACK, S], F32)
+        log_term = tile("log_term", [P, PACK, S], F32)
+        pres = tile("pres", [P, PACK, S], F32)
+
+        def w1_cast(h, copy):
+            copy(
+                w1_grouped[:, :, h * 64 : (h + 1) * 64, :].rearrange("p t m j -> p m j t"),
+                w1_raw[h][:].rearrange("p j (m t) -> p m j t", t=PACK),
+            )
+
+        def thickness_products():
+            w1_codes, w1_scales = quantize("w1q", w1_grouped[:].rearrange("p t m j -> p (t m j)"), H)
+            for t in range(PACK):
+                hi.append(bank(4 + t, "hi%d" % t))
+                mx(hi[t][:], (w1_codes[:, t * P : (t + 1) * P], w1_scales[:, t * P : (t + 1) * P]), xg)
+                nc.scalar.activation(exp_hi[:, t, :], hi[t][:], ACT.Exp)
+
+        def water():
+            nc.scalar.activation(open_water[:], owat_sb[:], ACT.Exp, scale=-1.0)
+
+        def logs():
+            for t in range(PACK):
+                nc.scalar.activation(log_term[:, t, :], exp_hi[:, t, :], ACT.Ln, bias=1.0)
+
+        def strength(t):
+            thk = tile("thk%d" % t, [P, S], F32)
+            nc.vector.scalar_tensor_tensor(thk[:], log_term[:, t, :], SOFTPLUS_LINEAR_FROM, hi[t][:], ALU.min, ALU.max)
+            nc.vector.scalar_tensor_tensor(
+                pres[:, t, :], thk[:], unit_sb[:, t : t + 1], open_water[:, t, :], ALU.mult, ALU.mult
+            )
+
+        result = tile("result", [P, S], F32)
+
+        def finish(c):
+            d2, num_t = sums[c]
+            cols = slice(c * P, (c + 1) * P)
+            inv_delta = tile("inv_delta%d" % c, [P, PACK, P], F32)
+            nc.scalar.activation(
+                inv_delta[:], d2[:].rearrange("j (p t) -> j t p", t=PACK), ACT.Abs_reciprocal_sqrt, bias=0.05
+            )
+            ratio_t = tile("ratio_t%d" % c, [P, PACK, P], F32)
+            nc.vector.tensor_tensor(
+                ratio_t[:], num_t[:].rearrange("j (p t) -> j t p", t=PACK), inv_delta[:], ALU.mult
+            )
+            ratio = bank(2 * c, "ratio%d" % c)
+            for t in range(PACK):
+                turn(ratio[:, t * P : (t + 1) * P], ratio_t[:, t, :], True, True)
+            hid = tile("hid%d" % c, [P, P * PACK], BF16)
+            nc.vector.scalar_tensor_tensor(
+                hid[:].rearrange("p (j t) -> p j t", t=PACK),
+                ratio[:].rearrange("p (t j) -> p j t", t=PACK),
+                -0.5,
+                pres[:, :, cols].rearrange("p t j -> p j t"),
+                ALU.add,
+                ALU.mult,
+            )
+            hid_codes, hid_scales = quantize("hidq%d" % c, hid[:], P)
+            modes = bank(2 * c + 1, "modes%d" % c)
+            mx(modes[:, 0:P], (w3_codes[:], w3_scales[:]), (hid_codes[:], hid_scales[:]))
+            nc.scalar.copy(result[:, cols], modes[:, 0:P])
+            nc.sync.dma_start(out[:, cols], result[:, cols])
+
+        w1_cast(0, nc.vector.tensor_copy)
+        w1_cast(1, nc.vector.tensor_copy)
+        thickness_products()
+        strains(0, 0, True)
+        strains(0, 1, True)
+        strains(0, 2, True)
+        strains(0, 3, False)
+        water()
+        logs()
+        strength(0)
+        strength(1)
+        strength(2)
+        strength(3)
+        strains(1, 0, False)
+        strains(1, 1, False)
+        strains(1, 2, False)
+        strains(1, 3, False)
+        squares(0, 0)
+        squares(0, 1)
+        squares(0, 2)
+        squares(0, 3)
+        turned_sums(0)
+        turned_sums(1)
+        w3_grouped = group_rows(nc.vector.tensor_copy, "w3_grouped", w3_raw[:], N)
+        w3_codes, w3_scales = quantize("w3q", w3_grouped[:], N)
+        squares(1, 0)
+        squares(1, 1)
+        squares(1, 2)
+        squares(1, 3)
+        turned_sums(2)
+        turned_sums(3)
+        finish(0)
+        finish(1)
+        finish(2)
+        finish(3)

@@ -18,7 +18,13 @@ ALU = mybir.AluOpType
 
 P = 128
 PACK = 4
+BLOCKS = H // P
 HALF = S // 2
+PIECES = 2 * BLOCKS
+NORTH_ON_SCALAR = 2
+SQUARES_BEFORE_LOG = 4
+COPY_BY_DMA_FROM = 2
+SQUARE_ON_VECTOR = 1
 SOFTPLUS_LINEAR_FROM = 40.0
 
 
@@ -30,13 +36,13 @@ def tile_picked_yseaic_str_p_kernel(
         sb = ctx.enter_context(tc.tile_pool(name="sb", bufs=1))
         psum = ctx.enter_context(tc.psum_pool(name="psum", bufs=1))
 
-        def tile(name, shape, dtype):
-            return sb.tile(shape, dtype, name=name, align_bytes=64)
+        def tile(name, shape, dtype, on_bytes_of=None):
+            return sb.tile(shape, dtype, name=name, tag=on_bytes_of or name, align_bytes=64)
 
         def bank(number, name):
             return psum.tile([P, 512], F32, name=name, tag="bank%d" % number)
 
-        def mx(dst, lhs, rhs):
+        def product(dst, lhs, rhs):
             nc.tensor.matmul_mx(
                 out=dst,
                 lhsT=lhs[0].bitcast(FP8X4),
@@ -51,7 +57,23 @@ def tile_picked_yseaic_str_p_kernel(
             codes = tile(name + "_codes", [P, width], U32)
             scales = tile(name + "_scales", [P, width], U8)
             nc.vector.quantize_mx(out=codes[:].bitcast(FP8X4), scales=scales[:], in_=grouped)
-            return codes, scales
+            return codes[:], scales[:]
+
+        def group_rows(copy, name, raw):
+            grouped = tile(name, [P, P * PACK], BF16)
+            copy(
+                grouped[:].rearrange("p (c e j) -> p c j e", e=2, j=PACK),
+                raw.rearrange("p j (c e) -> p c j e", e=2),
+            )
+            return grouped[:]
+
+        def turn(dst, src, start, stop):
+            nc.tensor.matmul(dst, src, ident[:], start=start, stop=stop, is_transpose=True)
+
+        def load_rows(name, weight, c0, c1):
+            raw = tile(name, [P, PACK, c1 - c0], F32)
+            nc.sync.dma_start(raw[:], weight.rearrange("(p j) c -> p j c", j=PACK)[:, :, c0:c1])
+            return raw
 
         offs_sb = tile("offs_sb", [P, S // 16], U16)
         est_sb = tile("est_sb", [P, S // 16], U16)
@@ -60,33 +82,18 @@ def tile_picked_yseaic_str_p_kernel(
         xs = tile("xs", [P, T], U8)
         nc.gpsimd.memset(xs[:].bitcast(I32), 0)
         nc.sync.dma_start(offs_sb[:], offs)
-        w2_view = w2.rearrange("(p j) c -> p j c", j=PACK)
-        w2_raw = []
-
-        def load_w2(number, c0, c1):
-            raw = tile("w2_raw%d" % number, [P, PACK, c1 - c0], F32)
-            nc.sync.dma_start(raw[:], w2_view[:, :, c0:c1])
-            for c in range(0, c1 - c0, P):
-                w2_raw.append(raw[:, :, c : c + P])
-
-        load_w2(0, 0, P)
+        w2_first = load_rows("w2_first", w2, 0, P)
         for q in range(4):
             nc.sync.dma_start(xs[32 * q : 32 * q + 4, :].bitcast(I32), x_scales[0, 4 * q : 4 * q + 4, :].bitcast(I32))
         nc.sync.dma_start(xw[:].bitcast(I32), x_words[0].rearrange("p n t -> p (n t)").bitcast(I32))
-        load_w2(1, P, 2 * P)
-        load_w2(2, 2 * P, H)
+        w2_second = load_rows("w2_second", w2, P, 2 * P)
+        w2_rest = load_rows("w2_rest", w2, 2 * P, H)
+        w2_raw = [w2_first[:], w2_second[:], w2_rest[:, :, 0:P], w2_rest[:, :, P : 2 * P]]
         nc.sync.dma_start(est_sb[:], est)
         nc.sync.dma_start(nor_sb[:], nor)
-        owat_sb = tile("owat_sb", [P, PACK, S], F32)
-        nc.sync.dma_start(owat_sb[:], owat.rearrange("(p t) j -> p t j", t=PACK))
-        w1_view = w1.rearrange("(p j) c -> p j c", j=PACK)
-        w1_raw = []
-        for h in range(2):
-            raw = tile("w1_raw%d" % h, [P, PACK, H // 2], F32)
-            nc.sync.dma_start(raw[:], w1_view[:, :, h * (H // 2) : (h + 1) * (H // 2)])
-            w1_raw.append(raw)
-        w3_raw = tile("w3_raw", [P, PACK, N], F32)
-        nc.sync.dma_start(w3_raw[:], w3.rearrange("(p j) c -> p j c", j=PACK))
+        w1_raw = [load_rows("w1_raw%d" % h, w1, h * (H // 2), (h + 1) * (H // 2)) for h in range(2)]
+        owat_sb = [load_rows("owat_sb%d" % h, owat, h * HALF, (h + 1) * HALF) for h in range(2)]
+        w3_raw = load_rows("w3_raw", w3, 0, N)
         unit_sb = tile("unit_sb", [P, PACK], F32)
         nc.sync.dma_start(unit_sb[:], unit.rearrange("(p t) o -> p (t o)", t=PACK))
 
@@ -99,169 +106,140 @@ def tile_picked_yseaic_str_p_kernel(
         nc.vector.tensor_copy(xg_codes[:], xw[:].indirect(offs_sb[:]))
         xg = (xg_codes[:], xg_scales[:])
 
-        def group_rows(engine_copy, name, raw, width):
-            grouped = tile(name, [P, width * PACK], BF16)
-            engine_copy(
-                grouped[:].rearrange("p (c e j) -> p c j e", e=2, j=PACK),
-                raw.rearrange("p j (c e) -> p c j e", e=2),
-            )
-            return grouped
-
-        uu, uu_copy = [], []
-        for b in range(4):
+        uu = []
+        for b in range(BLOCKS):
             copy = nc.scalar.copy if b == 0 else nc.vector.tensor_copy
-            grouped = group_rows(copy, "w2_grouped%d" % b, w2_raw[b], P)
-            codes, scales = quantize("w2q%d" % b, grouped[:], P)
+            w2q = quantize("w2q%d" % b, group_rows(copy, "w2_grouped%d" % b, w2_raw[b]), P)
             ui = bank(b, "ui%d" % b)
-            mx(ui[:], (codes[:], scales[:]), xg)
-            u = tile("uu%d" % b, [P, S], F32)
-            nc.scalar.activation(u[:], ui[:], ACT.Tanh)
-            u2 = tile("uu_copy%d" % b, [P, S], F32)
-            nc.vector.tensor_copy(u2[:], u[:])
-            uu.append(u)
-            uu_copy.append(u2)
+            product(ui[:], w2q, xg)
+            uu.append(tile("uu%d" % b, [P, S], F32))
+            nc.scalar.activation(uu[b][:], ui[:], ACT.Tanh)
 
-        def entries(h):
-            return slice(h * HALF // 16, (h + 1) * HALF // 16)
-
-        def strains(h, b, on_scalar):
-            cols = slice(h * HALF, (h + 1) * HALF)
-            epa = tile("epa%d_%d" % (h, b), [P, HALF], F32)
-            epb = tile("epb%d_%d" % (h, b), [P, HALF], F32)
-            nc.vector.tensor_tensor(epa[:], uu[b][:].indirect(est_sb[:, entries(h)]), uu_copy[b][:, cols], ALU.subtract)
-            if on_scalar:
-                un = tile("un%d_%d" % (h, b), [P, HALF], F32)
-                nc.scalar.activation(un[:], uu[b][:].indirect(nor_sb[:, entries(h)]), ACT.Copy, scale=0.375)
-                nc.vector.scalar_tensor_tensor(epb[:], uu[b][:, cols], -0.375, un[:], ALU.mult, ALU.add)
-                strain[h, b] = (epa, epb, 0.5 / 0.375, [epa, epb])
-                return
-            nc.vector.tensor_tensor(epb[:], uu[b][:].indirect(nor_sb[:, entries(h)]), uu_copy[b][:, cols], ALU.subtract)
-            num = tile("num%d_%d" % (h, b), [P, HALF], F32)
-            nc.vector.scalar_tensor_tensor(num[:], epb[:], 0.375, epa[:], ALU.mult, ALU.add)
-            strain[h, b] = (epa, epb, 0.5, [num])
-
-        def squares(h, b):
-            epa, epb, scale, terms = strain[h, b]
-            sqa = tile("sqa%d_%d" % (h, b), [P, HALF], F32)
-            sqb = tile("sqb%d_%d" % (h, b), [P, HALF], F32)
-            nc.scalar.activation(sqa[:], epa[:], ACT.Square)
-            nc.scalar.activation(sqb[:], epb[:], ACT.Square, scale=scale)
-            squared[h, b] = (sqa, sqb)
-
-        def turn(dst, src, start, stop):
-            nc.tensor.matmul(dst, src, ident[:], start=start, stop=stop, is_transpose=True)
-
-        def turned_sums(c):
-            h, cols = c // 2, slice((c % 2) * P, (c % 2 + 1) * P)
-            d2 = bank(2 * c, "d2_%d" % c)
-            num_t = bank(2 * c + 1, "num_t%d" % c)
-            for b in range(4):
-                terms = strain[h, b][3]
-                for number, term in enumerate(terms):
-                    turn(num_t[:, b * P : (b + 1) * P], term[:, cols], number == 0, number == len(terms) - 1)
-            for b in range(4):
-                sqa, sqb = squared[h, b]
-                turn(d2[:, b * P : (b + 1) * P], sqa[:, cols], True, False)
-                turn(d2[:, b * P : (b + 1) * P], sqb[:, cols], False, True)
-            sums.append((d2, num_t))
-
-        strain, squared, sums, hi = {}, {}, [], []
         w1_grouped = tile("w1_grouped", [P, PACK, P, PACK], BF16)
-        exp_hi = tile("exp_hi", [P, PACK, S], F32)
-        open_water = tile("open_water", [P, PACK, S], F32)
-        log_term = tile("log_term", [P, PACK, S], F32)
-        pres = tile("pres", [P, PACK, S], F32)
-
-        def w1_cast(h, copy):
-            copy(
+        for h in range(2):
+            nc.vector.tensor_copy(
                 w1_grouped[:, :, h * 64 : (h + 1) * 64, :].rearrange("p t m j -> p m j t"),
                 w1_raw[h][:].rearrange("p j (m t) -> p m j t", t=PACK),
             )
+        w1_codes, w1_scales = quantize("w1q", w1_grouped[:].rearrange("p t m j -> p (t m j)"), H)
+        hi, exp_hi = [], []
+        for t in range(PACK):
+            hi.append(bank(BLOCKS + t, "hi%d" % t))
+            product(hi[t][:], (w1_codes[:, t * P : (t + 1) * P], w1_scales[:, t * P : (t + 1) * P]), xg)
+            exp_hi.append(tile("exp_hi%d" % t, [P, S], F32))
+            nc.scalar.activation(exp_hi[t][:], hi[t][:], ACT.Exp)
 
-        def thickness_products():
-            w1_codes, w1_scales = quantize("w1q", w1_grouped[:].rearrange("p t m j -> p (t m j)"), H)
-            for t in range(PACK):
-                hi.append(bank(4 + t, "hi%d" % t))
-                mx(hi[t][:], (w1_codes[:, t * P : (t + 1) * P], w1_scales[:, t * P : (t + 1) * P]), xg)
-                nc.scalar.activation(exp_hi[:, t, :], hi[t][:], ACT.Exp)
+        own = []
+        own_by_vector = tile("own_by_vector", [P, COPY_BY_DMA_FROM, HALF], F32, "w1_raw1")
+        for piece in range(PIECES):
+            h, b = divmod(piece, BLOCKS)
+            if piece < COPY_BY_DMA_FROM:
+                own.append(own_by_vector[:, piece, :])
+            else:
+                own.append(tile("own%d" % piece, [P, HALF], F32)[:])
+                nc.sync.dma_start(own[piece], uu[b][:, h * HALF : (h + 1) * HALF])
+        north = tile("north", [P, NORTH_ON_SCALAR, HALF], F32, "w1_raw0")
+        strain = []
 
-        def water():
-            nc.scalar.activation(open_water[:], owat_sb[:], ACT.Exp, scale=-1.0)
+        def strains(piece, epa, epb):
+            h, b = divmod(piece, BLOCKS)
+            cols = slice(h * HALF, (h + 1) * HALF)
+            entries = slice(h * HALF // 16, (h + 1) * HALF // 16)
+            if piece < COPY_BY_DMA_FROM:
+                nc.vector.tensor_copy(own[piece], uu[b][:, cols])
+            nc.vector.tensor_tensor(epa, uu[b][:].indirect(est_sb[:, entries]), own[piece], ALU.subtract)
+            if piece < NORTH_ON_SCALAR:
+                nc.scalar.activation(north[:, piece, :], uu[b][:].indirect(nor_sb[:, entries]), ACT.Copy, scale=0.375)
+                nc.vector.scalar_tensor_tensor(epb, uu[b][:, cols], -0.375, north[:, piece, :], ALU.mult, ALU.add)
+                strain.append((epa, epb, 0.5 / 0.375, [epa, epb]))
+            else:
+                nc.vector.tensor_tensor(epb, uu[b][:].indirect(nor_sb[:, entries]), own[piece], ALU.subtract)
+                num = tile("num%d" % piece, [P, HALF], F32)
+                nc.vector.scalar_tensor_tensor(num[:], epb, 0.375, epa, ALU.mult, ALU.add)
+                strain.append((epa, epb, 0.5, [num[:]]))
 
-        def logs():
-            for t in range(PACK):
-                nc.scalar.activation(log_term[:, t, :], exp_hi[:, t, :], ACT.Ln, bias=1.0)
+        strain_tile = tile("strain_tile", [P, PIECES, 2, HALF], F32, "w1_grouped")
+        for piece in range(PIECES):
+            strains(piece, strain_tile[:, piece, 0, :], strain_tile[:, piece, 1, :])
 
-        def strength(t):
-            thk = tile("thk%d" % t, [P, S], F32)
-            nc.vector.scalar_tensor_tensor(thk[:], log_term[:, t, :], SOFTPLUS_LINEAR_FROM, hi[t][:], ALU.min, ALU.max)
+        squares = []
+
+        def square(piece, dst):
+            epa, epb, scale, terms = strain[piece]
+            if piece < PIECES - SQUARE_ON_VECTOR:
+                nc.scalar.activation(dst[:, 0, :], epa, ACT.Square)
+            else:
+                nc.vector.tensor_tensor(dst[:, 0, :], epa, epa, ALU.mult)
+            nc.scalar.activation(dst[:, 1, :], epb, ACT.Square, scale=scale)
+            squares.append(dst)
+
+        open_water = tile("open_water", [P, PACK, S], F32)
+        for h in range(2):
+            nc.scalar.activation(open_water[:, :, h * HALF : (h + 1) * HALF], owat_sb[h][:], ACT.Exp, scale=-1.0)
+        early_squares = tile("early_squares", [P, SQUARES_BEFORE_LOG, 2, HALF], F32, "owat_sb0")
+        for piece in range(SQUARES_BEFORE_LOG):
+            square(piece, early_squares[:, piece, :, :])
+        log_term = tile("log_term", [P, PACK, S], F32, "owat_sb1")
+        for t in range(PACK):
+            nc.scalar.activation(log_term[:, t, :], exp_hi[t][:], ACT.Ln, bias=1.0)
+        w3q = quantize("w3q", group_rows(nc.vector.tensor_copy, "w3_grouped", w3_raw[:]), N)
+        thk = []
+        for t in range(PACK):
+            thk.append(tile("thk%d" % t, [P, S], F32))
+            nc.vector.scalar_tensor_tensor(thk[t][:], log_term[:, t, :], SOFTPLUS_LINEAR_FROM, hi[t][:], ALU.min, ALU.max)
+
+        late_squares = tile("late_squares", [P, PIECES - SQUARES_BEFORE_LOG, 2, HALF], F32, "exp_hi2")
+        for piece in range(SQUARES_BEFORE_LOG, PIECES):
+            square(piece, late_squares[:, piece - SQUARES_BEFORE_LOG, :, :])
+
+        pres = tile("pres", [P, PACK, S], F32, "exp_hi3")
+        for t in range(PACK):
             nc.vector.scalar_tensor_tensor(
-                pres[:, t, :], thk[:], unit_sb[:, t : t + 1], open_water[:, t, :], ALU.mult, ALU.mult
+                pres[:, t, :], thk[t][:], unit_sb[:, t : t + 1], open_water[:, t, :], ALU.mult, ALU.mult
             )
 
-        result = tile("result", [P, S], F32)
+        delta2_t, num_t = [], []
+        for c in range(S // P):
+            h, cols = c // 2, slice((c % 2) * P, (c % 2 + 1) * P)
+            delta2_t.append(bank(2 * c, "delta2_t%d" % c))
+            num_t.append(bank(2 * c + 1, "num_t%d" % c))
+            for b in range(BLOCKS):
+                piece = h * BLOCKS + b
+                rows = slice(b * P, (b + 1) * P)
+                turn(delta2_t[c][:, rows], squares[piece][:, 0, cols], True, False)
+                turn(delta2_t[c][:, rows], squares[piece][:, 1, cols], False, True)
+                terms = strain[piece][3]
+                for number, term in enumerate(terms):
+                    turn(num_t[c][:, rows], term[:, cols], number == 0, number == len(terms) - 1)
 
-        def finish(c):
-            d2, num_t = sums[c]
-            cols = slice(c * P, (c + 1) * P)
+        ratio = []
+        for c in range(S // P):
             inv_delta = tile("inv_delta%d" % c, [P, PACK, P], F32)
             nc.scalar.activation(
-                inv_delta[:], d2[:].rearrange("j (p t) -> j t p", t=PACK), ACT.Abs_reciprocal_sqrt, bias=0.05
+                inv_delta[:], delta2_t[c][:].rearrange("j (p t) -> j t p", t=PACK), ACT.Abs_reciprocal_sqrt, bias=0.05
             )
             ratio_t = tile("ratio_t%d" % c, [P, PACK, P], F32)
             nc.vector.tensor_tensor(
-                ratio_t[:], num_t[:].rearrange("j (p t) -> j t p", t=PACK), inv_delta[:], ALU.mult
+                ratio_t[:], num_t[c][:].rearrange("j (p t) -> j t p", t=PACK), inv_delta[:], ALU.mult
             )
-            ratio = bank(2 * c, "ratio%d" % c)
+            ratio.append(bank(2 * c, "ratio%d" % c))
             for t in range(PACK):
-                turn(ratio[:, t * P : (t + 1) * P], ratio_t[:, t, :], True, True)
+                turn(ratio[c][:, t * P : (t + 1) * P], ratio_t[:, t, :], True, True)
+
+        result = tile("result", [P, S], F32)
+        for c in range(S // P):
+            cols = slice(c * P, (c + 1) * P)
             hid = tile("hid%d" % c, [P, P * PACK], BF16)
             nc.vector.scalar_tensor_tensor(
                 hid[:].rearrange("p (j t) -> p j t", t=PACK),
-                ratio[:].rearrange("p (t j) -> p j t", t=PACK),
+                ratio[c][:].rearrange("p (t j) -> p j t", t=PACK),
                 -0.5,
                 pres[:, :, cols].rearrange("p t j -> p j t"),
                 ALU.add,
                 ALU.mult,
             )
-            hid_codes, hid_scales = quantize("hidq%d" % c, hid[:], P)
+            hidq = quantize("hidq%d" % c, hid[:], P)
             modes = bank(2 * c + 1, "modes%d" % c)
-            mx(modes[:, 0:P], (w3_codes[:], w3_scales[:]), (hid_codes[:], hid_scales[:]))
+            product(modes[:, 0:P], w3q, hidq)
             nc.scalar.copy(result[:, cols], modes[:, 0:P])
             nc.sync.dma_start(out[:, cols], result[:, cols])
-
-        w1_cast(0, nc.vector.tensor_copy)
-        w1_cast(1, nc.vector.tensor_copy)
-        thickness_products()
-        strains(0, 0, True)
-        strains(0, 1, True)
-        strains(0, 2, True)
-        strains(0, 3, False)
-        water()
-        logs()
-        strength(0)
-        strength(1)
-        strength(2)
-        strength(3)
-        strains(1, 0, False)
-        strains(1, 1, False)
-        strains(1, 2, False)
-        strains(1, 3, False)
-        squares(0, 0)
-        squares(0, 1)
-        squares(0, 2)
-        squares(0, 3)
-        turned_sums(0)
-        turned_sums(1)
-        w3_grouped = group_rows(nc.vector.tensor_copy, "w3_grouped", w3_raw[:], N)
-        w3_codes, w3_scales = quantize("w3q", w3_grouped[:], N)
-        squares(1, 0)
-        squares(1, 1)
-        squares(1, 2)
-        squares(1, 3)
-        turned_sums(2)
-        turned_sums(3)
-        finish(0)
-        finish(1)
-        finish(2)
-        finish(3)

@@ -25,6 +25,8 @@ NORTH_ON_SCALAR = 2
 SQUARES_BEFORE_LOG = 4
 COPY_BY_DMA_FROM = 2
 SQUARE_ON_VECTOR = 1
+BEFORE_W1 = 0
+WOVEN_ON_SCALAR = 3
 SOFTPLUS_LINEAR_FROM = 40.0
 
 
@@ -59,8 +61,8 @@ def tile_picked_yseaic_str_p_kernel(
             nc.vector.quantize_mx(out=codes[:].bitcast(FP8X4), scales=scales[:], in_=grouped)
             return codes[:], scales[:]
 
-        def group_rows(copy, name, raw):
-            grouped = tile(name, [P, P * PACK], BF16)
+        def group_rows(copy, name, raw, on_bytes_of=None):
+            grouped = tile(name, [P, P * PACK], BF16, on_bytes_of)
             copy(
                 grouped[:].rearrange("p (c e j) -> p c j e", e=2, j=PACK),
                 raw.rearrange("p j (c e) -> p c j e", e=2),
@@ -83,8 +85,8 @@ def tile_picked_yseaic_str_p_kernel(
         nc.gpsimd.memset(xs[:].bitcast(I32), 0)
         nc.sync.dma_start(offs_sb[:], offs)
         w2_first = load_rows("w2_first", w2, 0, P)
-        for q in range(4):
-            nc.sync.dma_start(xs[32 * q : 32 * q + 4, :].bitcast(I32), x_scales[0, 4 * q : 4 * q + 4, :].bitcast(I32))
+        for r in range(4):
+            nc.sync.dma_start(xs[r:P:32, :].bitcast(I32), x_scales[0, r:16:4, :].bitcast(I32))
         nc.sync.dma_start(xw[:].bitcast(I32), x_words[0].rearrange("p n t -> p (n t)").bitcast(I32))
         w2_second = load_rows("w2_second", w2, P, 2 * P)
         w2_rest = load_rows("w2_rest", w2, 2 * P, H)
@@ -92,7 +94,10 @@ def tile_picked_yseaic_str_p_kernel(
         nc.sync.dma_start(est_sb[:], est)
         nc.sync.dma_start(nor_sb[:], nor)
         w1_raw = [load_rows("w1_raw%d" % h, w1, h * (H // 2), (h + 1) * (H // 2)) for h in range(2)]
-        owat_sb = [load_rows("owat_sb%d" % h, owat, h * HALF, (h + 1) * HALF) for h in range(2)]
+        owat_sb = []
+        for h in range(2):
+            owat_sb.append(tile("owat_sb%d" % h, [P, 2, S], F32))
+            nc.sync.dma_start(owat_sb[h][:], owat.rearrange("(p t) j -> p t j", t=PACK)[:, 2 * h : 2 * h + 2, :])
         w3_raw = load_rows("w3_raw", w3, 0, N)
         unit_sb = tile("unit_sb", [P, PACK], F32)
         nc.sync.dma_start(unit_sb[:], unit.rearrange("(p t) o -> p (t o)", t=PACK))
@@ -108,7 +113,7 @@ def tile_picked_yseaic_str_p_kernel(
 
         uu = []
         for b in range(BLOCKS):
-            copy = nc.scalar.copy if b == 0 else nc.vector.tensor_copy
+            copy = nc.scalar.copy if b < 1 else nc.vector.tensor_copy
             w2q = quantize("w2q%d" % b, group_rows(copy, "w2_grouped%d" % b, w2_raw[b]), P)
             ui = bank(b, "ui%d" % b)
             product(ui[:], w2q, xg)
@@ -130,7 +135,7 @@ def tile_picked_yseaic_str_p_kernel(
             nc.scalar.activation(exp_hi[t][:], hi[t][:], ACT.Exp)
 
         own = []
-        own_by_vector = tile("own_by_vector", [P, COPY_BY_DMA_FROM, HALF], F32, "w1_raw1")
+        own_by_vector = tile("own_by_vector", [P, COPY_BY_DMA_FROM, HALF], F32, "w2_grouped3")
         for piece in range(PIECES):
             h, b = divmod(piece, BLOCKS)
             if piece < COPY_BY_DMA_FROM:
@@ -138,7 +143,7 @@ def tile_picked_yseaic_str_p_kernel(
             else:
                 own.append(tile("own%d" % piece, [P, HALF], F32)[:])
                 nc.sync.dma_start(own[piece], uu[b][:, h * HALF : (h + 1) * HALF])
-        north = tile("north", [P, NORTH_ON_SCALAR, HALF], F32, "w1_raw0")
+        north = tile("north", [P, NORTH_ON_SCALAR, HALF], F32, "w2q3_scales")
         strain = []
 
         def strains(piece, epa, epb):
@@ -158,9 +163,9 @@ def tile_picked_yseaic_str_p_kernel(
                 nc.vector.scalar_tensor_tensor(num[:], epb, 0.375, epa, ALU.mult, ALU.add)
                 strain.append((epa, epb, 0.5, [num[:]]))
 
-        strain_tile = tile("strain_tile", [P, PIECES, 2, HALF], F32, "w1_grouped")
-        for piece in range(PIECES):
-            strains(piece, strain_tile[:, piece, 0, :], strain_tile[:, piece, 1, :])
+        strain_tile = tile("strain_tile", [P, PIECES - BEFORE_W1, 2, HALF], F32, "w1_grouped")
+        for piece in range(BEFORE_W1, PIECES):
+            strains(piece, strain_tile[:, piece - BEFORE_W1, 0, :], strain_tile[:, piece - BEFORE_W1, 1, :])
 
         squares = []
 
@@ -173,16 +178,15 @@ def tile_picked_yseaic_str_p_kernel(
             nc.scalar.activation(dst[:, 1, :], epb, ACT.Square, scale=scale)
             squares.append(dst)
 
-        open_water = tile("open_water", [P, PACK, S], F32)
+        open_water = tile("open_water", [P, PACK, S], F32, "w2q3_codes")
         for h in range(2):
-            nc.scalar.activation(open_water[:, :, h * HALF : (h + 1) * HALF], owat_sb[h][:], ACT.Exp, scale=-1.0)
+            nc.scalar.activation(open_water[:, 2 * h : 2 * h + 2, :], owat_sb[h][:], ACT.Exp, scale=-1.0)
         early_squares = tile("early_squares", [P, SQUARES_BEFORE_LOG, 2, HALF], F32, "owat_sb0")
         for piece in range(SQUARES_BEFORE_LOG):
             square(piece, early_squares[:, piece, :, :])
         log_term = tile("log_term", [P, PACK, S], F32, "owat_sb1")
         for t in range(PACK):
             nc.scalar.activation(log_term[:, t, :], exp_hi[t][:], ACT.Ln, bias=1.0)
-        w3q = quantize("w3q", group_rows(nc.vector.tensor_copy, "w3_grouped", w3_raw[:]), N)
         thk = []
         for t in range(PACK):
             thk.append(tile("thk%d" % t, [P, S], F32))
@@ -226,18 +230,29 @@ def tile_picked_yseaic_str_p_kernel(
             for t in range(PACK):
                 turn(ratio[c][:, t * P : (t + 1) * P], ratio_t[:, t, :], True, True)
 
+        w3q = quantize("w3q", group_rows(nc.scalar.copy, "w3_grouped", w3_raw[:], "exp_hi2"), N)
         result = tile("result", [P, S], F32)
         for c in range(S // P):
             cols = slice(c * P, (c + 1) * P)
             hid = tile("hid%d" % c, [P, P * PACK], BF16)
-            nc.vector.scalar_tensor_tensor(
-                hid[:].rearrange("p (j t) -> p j t", t=PACK),
-                ratio[c][:].rearrange("p (t j) -> p j t", t=PACK),
-                -0.5,
-                pres[:, :, cols].rearrange("p t j -> p j t"),
-                ALU.add,
-                ALU.mult,
-            )
+            if c < WOVEN_ON_SCALAR:
+                planes = tile("planes%d" % c, [P, PACK, P], BF16)
+                nc.vector.scalar_tensor_tensor(
+                    planes[:], ratio[c][:].rearrange("p (t j) -> p t j", t=PACK), -0.5, pres[:, :, cols], ALU.add, ALU.mult
+                )
+                nc.scalar.copy(
+                    hid[:].rearrange("p (g i t) -> p g t i", i=4, t=PACK),
+                    planes[:].rearrange("p t (g i) -> p g t i", i=4),
+                )
+            else:
+                nc.vector.scalar_tensor_tensor(
+                    hid[:].rearrange("p (j t) -> p j t", t=PACK),
+                    ratio[c][:].rearrange("p (t j) -> p j t", t=PACK),
+                    -0.5,
+                    pres[:, :, cols].rearrange("p t j -> p j t"),
+                    ALU.add,
+                    ALU.mult,
+                )
             hidq = quantize("hidq%d" % c, hid[:], P)
             modes = bank(2 * c + 1, "modes%d" % c)
             product(modes[:, 0:P], w3q, hidq)

@@ -114,7 +114,9 @@ def tile_picked_yseaic_str_p_kernel(
         uu = []
         for b in range(BLOCKS):
             copy = nc.scalar.copy if b < 1 else nc.vector.tensor_copy
-            w2q = quantize("w2q%d" % b, group_rows(copy, "w2_grouped%d" % b, w2_raw[b]), P)
+            grouped = tile("w2_grouped%d" % b, [P, PACK, P // PACK, PACK], BF16)
+            copy(grouped[:].rearrange("p t m j -> p m j t"), w2_raw[b].rearrange("p j (m t) -> p m j t", t=PACK))
+            w2q = quantize("w2q%d" % b, grouped[:].rearrange("p t m j -> p (t m j)"), P)
             ui = bank(b, "ui%d" % b)
             product(ui[:], w2q, xg)
             uu.append(tile("uu%d" % b, [P, S], F32))
@@ -220,11 +222,17 @@ def tile_picked_yseaic_str_p_kernel(
         for c in range(S // P):
             inv_delta = tile("inv_delta%d" % c, [P, PACK, P], F32)
             nc.scalar.activation(
-                inv_delta[:], delta2_t[c][:].rearrange("j (p t) -> j t p", t=PACK), ACT.Abs_reciprocal_sqrt, bias=0.05
+                inv_delta[:].rearrange("j t (b m) -> j t b m", b=BLOCKS),
+                delta2_t[c][:].rearrange("j (b t m) -> j t b m", b=BLOCKS, t=PACK),
+                ACT.Abs_reciprocal_sqrt,
+                bias=0.05,
             )
             ratio_t = tile("ratio_t%d" % c, [P, PACK, P], F32)
             nc.vector.tensor_tensor(
-                ratio_t[:], num_t[c][:].rearrange("j (p t) -> j t p", t=PACK), inv_delta[:], ALU.mult
+                ratio_t[:].rearrange("j t (b m) -> j t b m", b=BLOCKS),
+                num_t[c][:].rearrange("j (b t m) -> j t b m", b=BLOCKS, t=PACK),
+                inv_delta[:].rearrange("j t (b m) -> j t b m", b=BLOCKS),
+                ALU.mult,
             )
             ratio.append(bank(2 * c, "ratio%d" % c))
             for t in range(PACK):

from contextlib import ExitStack

import concourse.mybir as mybir
from concourse.masks import make_identity

K, T, S, N, H = 512, 2048, 512, 128, 512
FLOPS = 2 * K * H * S * 2 + 2 * H * N * S

F32 = mybir.dt.float32
BF16 = mybir.dt.bfloat16
I32 = mybir.dt.int32
U32 = mybir.dt.uint32
U16 = mybir.dt.uint16
U8 = mybir.dt.uint8
FP8X4 = mybir.dt.float8_e4m3fn_x4
ACT = mybir.ActivationFunctionType
ALU = mybir.AluOpType

P = 128
PACK = 4
BLOCKS = H // P
HALF = S // 2
PIECES = 2 * BLOCKS
NORTH_ON_SCALAR = 2
SQUARES_BEFORE_LOG = 4
COPY_BY_DMA_FROM = 2
SQUARE_ON_VECTOR = 1
BEFORE_W1 = 0
WOVEN_ON_SCALAR = 3
SOFTPLUS_LINEAR_FROM = 40.0


def tile_picked_yseaic_str_p_kernel(
    tc, x_words, x_scales, w1, w2, owat, unit, w3, offs, est, nor, out
):
    nc = tc.nc
    with ExitStack() as ctx:
        sb = ctx.enter_context(tc.tile_pool(name="sb", bufs=1))
        psum = ctx.enter_context(tc.psum_pool(name="psum", bufs=1))

        def tile(name, shape, dtype, on_bytes_of=None):
            return sb.tile(shape, dtype, name=name, tag=on_bytes_of or name, align_bytes=64)

        def bank(number, name):
            return psum.tile([P, 512], F32, name=name, tag="bank%d" % number)

        def product(dst, lhs, rhs):
            nc.tensor.matmul_mx(
                out=dst,
                lhsT=lhs[0].bitcast(FP8X4),
                lhsT_scale=lhs[1],
                rhs=rhs[0].bitcast(FP8X4),
                rhs_scale=rhs[1],
                start=True,
                stop=True,
            )

        def quantize(name, grouped, width):
            codes = tile(name + "_codes", [P, width], U32)
            scales = tile(name + "_scales", [P, width], U8)
            nc.vector.quantize_mx(out=codes[:].bitcast(FP8X4), scales=scales[:], in_=grouped)
            return codes[:], scales[:]

        def group_rows(copy, name, raw, on_bytes_of=None):
            grouped = tile(name, [P, P * PACK], BF16, on_bytes_of)
            copy(
                grouped[:].rearrange("p (c e j) -> p c j e", e=2, j=PACK),
                raw.rearrange("p j (c e) -> p c j e", e=2),
            )
            return grouped[:]

        def turn(dst, src, start, stop):
            nc.tensor.matmul(dst, src, ident[:], start=start, stop=stop, is_transpose=True)

        def load_rows(name, weight, c0, c1):
            raw = tile(name, [P, PACK, c1 - c0], F32)
            nc.sync.dma_start(raw[:], weight.rearrange("(p j) c -> p j c", j=PACK)[:, :, c0:c1])
            return raw

        offs_sb = tile("offs_sb", [P, S // 16], U16)
        est_sb = tile("est_sb", [P, S // 16], U16)
        nor_sb = tile("nor_sb", [P, S // 16], U16)
        xw = tile("xw", [P, T], U32)
        xs = tile("xs", [P, T], U8)
        nc.gpsimd.memset(xs[:].bitcast(I32), 0)
        nc.sync.dma_start(offs_sb[:], offs)
        w2_first = load_rows("w2_first", w2, 0, P)
        for r in range(4):
            nc.sync.dma_start(xs[r:P:32, :].bitcast(I32), x_scales[0, r:16:4, :].bitcast(I32))
        nc.sync.dma_start(xw[:].bitcast(I32), x_words[0].rearrange("p n t -> p (n t)").bitcast(I32))
        w2_second = load_rows("w2_second", w2, P, 2 * P)
        w2_rest = load_rows("w2_rest", w2, 2 * P, H)
        w2_raw = [w2_first[:], w2_second[:], w2_rest[:, :, 0:P], w2_rest[:, :, P : 2 * P]]
        nc.sync.dma_start(est_sb[:], est)
        nc.sync.dma_start(nor_sb[:], nor)
        w1_raw = [load_rows("w1_raw%d" % h, w1, h * (H // 2), (h + 1) * (H // 2)) for h in range(2)]
        owat_sb = []
        for h in range(2):
            owat_sb.append(tile("owat_sb%d" % h, [P, 2, S], F32))
            nc.sync.dma_start(owat_sb[h][:], owat.rearrange("(p t) j -> p t j", t=PACK)[:, 2 * h : 2 * h + 2, :])
        w3_raw = load_rows("w3_raw", w3, 0, N)
        unit_sb = tile("unit_sb", [P, PACK], F32)
        nc.sync.dma_start(unit_sb[:], unit.rearrange("(p t) o -> p (t o)", t=PACK))

        ident = tile("ident", [P, P], F32)
        make_identity(nc, ident[:])

        xg_scales = tile("xg_scales", [P, S], U8)
        xg_codes = tile("xg_codes", [P, S], U32)
        nc.vector.tensor_copy(xg_scales[:], xs[:].indirect(offs_sb[:]))
        nc.vector.tensor_copy(xg_codes[:], xw[:].indirect(offs_sb[:]))
        xg = (xg_codes[:], xg_scales[:])

        uu = []
        for b in range(BLOCKS):
            copy = nc.scalar.copy if b < 1 else nc.vector.tensor_copy
            grouped = tile("w2_grouped%d" % b, [P, PACK, P // PACK, PACK], BF16)
            copy(grouped[:].rearrange("p t m j -> p m j t"), w2_raw[b].rearrange("p j (m t) -> p m j t", t=PACK))
            w2q = quantize("w2q%d" % b, grouped[:].rearrange("p t m j -> p (t m j)"), P)
            ui = bank(b, "ui%d" % b)
            product(ui[:], w2q, xg)
            uu.append(tile("uu%d" % b, [P, S], F32))
            nc.scalar.activation(uu[b][:], ui[:], ACT.Tanh)

        w1_grouped = tile("w1_grouped", [P, PACK, P, PACK], BF16)
        for h in range(2):
            nc.vector.tensor_copy(
                w1_grouped[:, :, h * 64 : (h + 1) * 64, :].rearrange("p t m j -> p m j t"),
                w1_raw[h][:].rearrange("p j (m t) -> p m j t", t=PACK),
            )
        w1_codes, w1_scales = quantize("w1q", w1_grouped[:].rearrange("p t m j -> p (t m j)"), H)
        hi, exp_hi = [], []
        for t in range(PACK):
            hi.append(bank(BLOCKS + t, "hi%d" % t))
            product(hi[t][:], (w1_codes[:, t * P : (t + 1) * P], w1_scales[:, t * P : (t + 1) * P]), xg)
            exp_hi.append(tile("exp_hi%d" % t, [P, S], F32))
            nc.scalar.activation(exp_hi[t][:], hi[t][:], ACT.Exp)

        own = []
        own_by_vector = tile("own_by_vector", [P, COPY_BY_DMA_FROM, HALF], F32, "w2_grouped3")
        for piece in range(PIECES):
            h, b = divmod(piece, BLOCKS)
            if piece < COPY_BY_DMA_FROM:
                own.append(own_by_vector[:, piece, :])
            else:
                own.append(tile("own%d" % piece, [P, HALF], F32)[:])
                nc.sync.dma_start(own[piece], uu[b][:, h * HALF : (h + 1) * HALF])
        north = tile("north", [P, NORTH_ON_SCALAR, HALF], F32, "w2q3_scales")
        strain = []

        def strains(piece, epa, epb):
            h, b = divmod(piece, BLOCKS)
            cols = slice(h * HALF, (h + 1) * HALF)
            entries = slice(h * HALF // 16, (h + 1) * HALF // 16)
            if piece < COPY_BY_DMA_FROM:
                nc.vector.tensor_copy(own[piece], uu[b][:, cols])
            nc.vector.tensor_tensor(epa, uu[b][:].indirect(est_sb[:, entries]), own[piece], ALU.subtract)
            if piece < NORTH_ON_SCALAR:
                nc.scalar.activation(north[:, piece, :], uu[b][:].indirect(nor_sb[:, entries]), ACT.Copy, scale=0.375)
                nc.vector.scalar_tensor_tensor(epb, uu[b][:, cols], -0.375, north[:, piece, :], ALU.mult, ALU.add)
                strain.append((epa, epb, 0.5 / 0.375, [epa, epb]))
            else:
                nc.vector.tensor_tensor(epb, uu[b][:].indirect(nor_sb[:, entries]), own[piece], ALU.subtract)
                num = tile("num%d" % piece, [P, HALF], F32)
                nc.vector.scalar_tensor_tensor(num[:], epb, 0.375, epa, ALU.mult, ALU.add)
                strain.append((epa, epb, 0.5, [num[:]]))

        strain_tile = tile("strain_tile", [P, PIECES - BEFORE_W1, 2, HALF], F32, "w1_grouped")
        for piece in range(BEFORE_W1, PIECES):
            strains(piece, strain_tile[:, piece - BEFORE_W1, 0, :], strain_tile[:, piece - BEFORE_W1, 1, :])

        squares = []

        def square(piece, dst):
            epa, epb, scale, terms = strain[piece]
            if piece < PIECES - SQUARE_ON_VECTOR:
                nc.scalar.activation(dst[:, 0, :], epa, ACT.Square)
            else:
                nc.vector.tensor_tensor(dst[:, 0, :], epa, epa, ALU.mult)
            nc.scalar.activation(dst[:, 1, :], epb, ACT.Square, scale=scale)
            squares.append(dst)

        open_water = tile("open_water", [P, PACK, S], F32, "w2q3_codes")
        for h in range(2):
            nc.scalar.activation(open_water[:, 2 * h : 2 * h + 2, :], owat_sb[h][:], ACT.Exp, scale=-1.0)
        early_squares = tile("early_squares", [P, SQUARES_BEFORE_LOG, 2, HALF], F32, "owat_sb0")
        for piece in range(SQUARES_BEFORE_LOG):
            square(piece, early_squares[:, piece, :, :])
        log_term = tile("log_term", [P, PACK, S], F32, "owat_sb1")
        for t in range(PACK):
            nc.scalar.activation(log_term[:, t, :], exp_hi[t][:], ACT.Ln, bias=1.0)
        thk = []
        for t in range(PACK):
            thk.append(tile("thk%d" % t, [P, S], F32))
            nc.vector.scalar_tensor_tensor(thk[t][:], log_term[:, t, :], SOFTPLUS_LINEAR_FROM, hi[t][:], ALU.min, ALU.max)

        late_squares = tile("late_squares", [P, PIECES - SQUARES_BEFORE_LOG, 2, HALF], F32, "exp_hi2")
        for piece in range(SQUARES_BEFORE_LOG, PIECES):
            square(piece, late_squares[:, piece - SQUARES_BEFORE_LOG, :, :])

        pres = tile("pres", [P, PACK, S], F32, "exp_hi3")
        for t in range(PACK):
            nc.vector.scalar_tensor_tensor(
                pres[:, t, :], thk[t][:], unit_sb[:, t : t + 1], open_water[:, t, :], ALU.mult, ALU.mult
            )

        delta2_t, num_t = [], []
        for c in range(S // P):
            h, cols = c // 2, slice((c % 2) * P, (c % 2 + 1) * P)
            delta2_t.append(bank(2 * c, "delta2_t%d" % c))
            num_t.append(bank(2 * c + 1, "num_t%d" % c))
            for b in range(BLOCKS):
                piece = h * BLOCKS + b
                rows = slice(b * P, (b + 1) * P)
                turn(delta2_t[c][:, rows], squares[piece][:, 0, cols], True, False)
                turn(delta2_t[c][:, rows], squares[piece][:, 1, cols], False, True)
                terms = strain[piece][3]
                for number, term in enumerate(terms):
                    turn(num_t[c][:, rows], term[:, cols], number == 0, number == len(terms) - 1)

        ratio = []
        for c in range(S // P):
            inv_delta = tile("inv_delta%d" % c, [P, PACK, P], F32)
            nc.scalar.activation(
                inv_delta[:].rearrange("j t (b m) -> j t b m", b=BLOCKS),
                delta2_t[c][:].rearrange("j (b t m) -> j t b m", b=BLOCKS, t=PACK),
                ACT.Abs_reciprocal_sqrt,
                bias=0.05,
            )
            ratio_t = tile("ratio_t%d" % c, [P, PACK, P], F32)
            nc.vector.tensor_tensor(
                ratio_t[:].rearrange("j t (b m) -> j t b m", b=BLOCKS),
                num_t[c][:].rearrange("j (b t m) -> j t b m", b=BLOCKS, t=PACK),
                inv_delta[:].rearrange("j t (b m) -> j t b m", b=BLOCKS),
                ALU.mult,
            )
            ratio.append(bank(2 * c, "ratio%d" % c))
            for t in range(PACK):
                turn(ratio[c][:, t * P : (t + 1) * P], ratio_t[:, t, :], True, True)

        w3q = quantize("w3q", group_rows(nc.scalar.copy, "w3_grouped", w3_raw[:], "exp_hi2"), N)
        result = tile("result", [P, S], F32)
        for c in range(S // P):
            cols = slice(c * P, (c + 1) * P)
            hid = tile("hid%d" % c, [P, P * PACK], BF16)
            if c < WOVEN_ON_SCALAR:
                planes = tile("planes%d" % c, [P, PACK, P], BF16)
                nc.vector.scalar_tensor_tensor(
                    planes[:], ratio[c][:].rearrange("p (t j) -> p t j", t=PACK), -0.5, pres[:, :, cols], ALU.add, ALU.mult
                )
                nc.scalar.copy(
                    hid[:].rearrange("p (g i t) -> p g t i", i=4, t=PACK),
                    planes[:].rearrange("p t (g i) -> p g t i", i=4),
                )
            else:
                nc.vector.scalar_tensor_tensor(
                    hid[:].rearrange("p (j t) -> p j t", t=PACK),
                    ratio[c][:].rearrange("p (t j) -> p j t", t=PACK),
                    -0.5,
                    pres[:, :, cols].rearrange("p t j -> p j t"),
                    ALU.add,
                    ALU.mult,
                )
            hidq = quantize("hidq%d" % c, hid[:], P)
            modes = bank(2 * c + 1, "modes%d" % c)
            product(modes[:, 0:P], w3q, hidq)
            nc.scalar.copy(result[:, cols], modes[:, 0:P])
            nc.sync.dma_start(out[:, cols], result[:, cols])
